import numpy as np
import ml_dtypes


def mxq(x, axis, fmt="e4m3"):
    dtype, down = {"e4m3": (ml_dtypes.float8_e4m3fn, 7), "e5m2": (ml_dtypes.float8_e5m2, 14)}[fmt]
    v = np.moveaxis(np.asarray(x, np.float32).astype(ml_dtypes.bfloat16).astype(np.float64), axis, -1)
    blocks = v.reshape(v.shape[:-1] + (-1, 32))
    amax = np.abs(blocks).max(-1, keepdims=True)
    byte = np.maximum(np.where(amax > 0, np.frexp(amax)[1] - 1 + 127, 0) - down, 1)
    scale = np.exp2(byte - 127.0)
    codes = (blocks / scale).astype(np.float32).astype(dtype).astype(np.float64)
    return np.moveaxis((codes * scale).reshape(v.shape), -1, axis)


WIDE = False


def mx_kscale(k):
    if not WIDE:
        return np.ones(k)
    levels = np.array([10, -10, 5, -5, 0])
    if k % 512:
        return np.exp2(np.random.permutation(np.resize(levels, k // 32))).repeat(32)
    a = np.empty((k // 512, 16))
    for p in range(k // 512):
        a[p, :8] = np.random.permutation(np.resize(levels, 8))
        for g in range(8):
            far = levels[np.abs(levels - a[p, g]) >= 10]
            a[p, g + 8] = far[np.random.randint(len(far))]
    return np.exp2(a.ravel()).repeat(32)


def f64(x):
    return np.asarray(x).astype(np.float64)


def striped(idx):
    return np.tile(idx.reshape(-1, 16).T, (8, 1)).astype(np.uint16)


def unstriped(offs):
    return offs[:16].T.reshape(-1).astype(np.int64)


E2M1 = np.array([0.0, 0.5, 1.0, 1.5, 2.0, 3.0, 4.0, 6.0, -0.0, -0.5, -1.0, -1.5, -2.0, -3.0, -4.0, -6.0])


def pack_weight(w, fmt):
    k, n = w.shape
    w = f64(np.asarray(w, np.float32).astype(ml_dtypes.bfloat16)).reshape(k // 32, 32, n)
    amax = np.abs(w).max(1)
    if fmt == "e4m3":
        byte = np.frexp(amax)[1] - 1 + 127 - 7
    else:
        mant, ex = np.frexp(amax / 6.0)
        byte = np.where(mant > 0.5, ex, ex - 1) + 127
    byte = np.clip(np.where(amax > 0, byte, 1), 1, 254)
    scaled = (w * np.exp2(127.0 - byte)[:, None, :]).reshape(k, n).astype(np.float32)
    by_word = np.ascontiguousarray(scaled.reshape(k // 512, 128, 4, n).transpose(0, 1, 3, 2))
    if fmt == "e4m3":
        words = by_word.astype(ml_dtypes.float8_e4m3fn).view(np.uint8)
    else:
        c = by_word.astype(ml_dtypes.float4_e2m1fn).view(np.uint8) & 0xF
        words = (c[..., 0::2] | (c[..., 1::2] << 4)).reshape(k // 512, 128, 2 * n)
    return np.ascontiguousarray(words), np.ascontiguousarray(byte.astype(np.uint8).reshape(k // 512, 16, n))


def unpack_weight(words, scales, fmt):
    g, _, n = scales.shape
    words = np.ascontiguousarray(words).reshape(g, 128, n, -1)
    if fmt == "e4m3":
        vals = words.view(ml_dtypes.float8_e4m3fn).astype(np.float64)
    else:
        nib = np.empty((g, 128, n, 4), np.uint8)
        nib[..., 0::2] = words & 0xF
        nib[..., 1::2] = words >> 4
        vals = E2M1[nib]
    vals = vals * np.repeat(np.exp2(scales.astype(np.float64) - 127.0), 8, axis=1)[..., None]
    return vals.transpose(0, 1, 3, 2).reshape(g * 512, n)


def gelu(v):
    return 0.5 * v * (1.0 + np.tanh(np.sqrt(2.0 / np.pi) * (v + 0.044715 * v**3)))


K, M, H, T, S, T2, P = 1536, 512, 1024, 4096, 1024, 2048, 512

def setup_inputs():
    n = np.random.standard_normal
    s, u1, u = mx_kscale(K)[:, None], mx_kscale(M)[:, None], mx_kscale(H)[:, None]
    d = {}
    d["tab_words"], d["tab_scales"] = pack_weight(n((K, T)) * s, "e4m3")
    d["offs"] = striped(np.random.permutation(T)[:S])
    d["offs2"] = striped(np.random.permutation(T2)[:S])
    d["offs3"] = striped(np.random.permutation(T2)[:P])
    d["offs4"] = striped(np.random.permutation(T2)[:P])
    d["w1"] = (1.6 * n((K, M)) / K ** 0.5 / s).astype(np.float32)
    d["g1"] = (np.exp(0.3 * n(M)) * u1[:, 0]).astype(np.float32)
    d["w2_words"], d["w2_scales"] = pack_weight(1.4 * n((M, H)) / M ** 0.5 / u1 * u.T, "e2m1")
    d["wgs"] = np.exp(0.3 * n((128, S))).astype(np.float32)
    d["page0"] = (n((H, T2)) * u).astype(np.float32)
    d["gs"] = (1.5 * np.exp(0.3 * n(H)) / u[:, 0]).astype(np.float32)
    d["gp"] = (np.exp(0.3 * n(H)) * u[:, 0]).astype(np.float32)
    d["w3"] = (n((H, H)) / H ** 0.5 / u).astype(np.float32)
    d["gl"] = (np.exp(0.3 * n(H)) / u[:, 0]).astype(np.float32)
    return d

def reference(tab_words, tab_scales, offs, offs2, offs3, offs4, w1, g1, w2_words, w2_scales, wgs, page0, gs, gp, w3, gl):
    v = unpack_weight(tab_words, tab_scales, "e4m3")[:, unstriped(offs)]
    w2 = unpack_weight(w2_words, w2_scales, "e2m1")
    f = np.tanh(mxq(f64(w1), 0, "e4m3").T @ v) * f64(g1)[:, None]
    h = w2.T @ mxq(f, 0, "e4m3")
    page = f64(page0).copy()
    page[:, unstriped(offs2)] = np.tile(f64(wgs), (H // 128, 1)) * h
    r = page[:, unstriped(offs3)] * f64(gs)[:, None]
    x = r / (1.0 + np.exp(-r)) * f64(gp)[:, None]
    y = mxq(f64(w3), 0, "e4m3").T @ mxq(x, 0, "e4m3")
    settled = page[:, unstriped(offs4)] * f64(gl)[:, None]
    return np.minimum(y, settled)

from contextlib import ExitStack

import concourse.mybir as mybir

K, M, H, T, S, T2, PICK = 1536, 512, 1024, 4096, 1024, 2048, 512
FLOPS = 2 * (K * M * S + M * H * S + H * H * PICK)

F32 = mybir.dt.float32
BF16 = mybir.dt.bfloat16
I32 = mybir.dt.int32
U32 = mybir.dt.uint32
U16 = mybir.dt.uint16
U8 = mybir.dt.uint8
FP8X4 = mybir.dt.float8_e4m3fn_x4
FP4X4 = mybir.dt.float4_e2m1fn_x4
ACT = mybir.ActivationFunctionType
ALU = mybir.AluOpType

P = 128
PACK = 4
PASS = P * PACK
HALF = S // 2
PIECE = 128
PER_COL = 16
ORDER = [(0, 0), (1, 0), (0, 1), (0, 2), (0, 3), (1, 1), (1, 2), (1, 3)]


def tile_list_ring_pressure_board_kernel(
    tc, tab_words, tab_scales, offs, offs2, offs3, offs4, w1, g1, w2_words, w2_scales, wgs, page0, gs, gp, w3, gl, out
):
    nc = tc.nc
    with ExitStack() as ctx:
        lists = ctx.enter_context(tc.tile_pool(name="lists", bufs=1))
        sb = ctx.enter_context(tc.tile_pool(name="sb", bufs=1))
        arena = ctx.enter_context(tc.tile_pool(name="arena", bufs=1))
        psum = ctx.enter_context(tc.psum_pool(name="psum", bufs=1))

        def tile(shape, dtype, name, tag=None, bufs=1):
            return sb.tile(shape, dtype, name=name, tag=tag or name, bufs=bufs, align_bytes=64)

        def placed(shape, dtype, name, kib):
            return arena.tile(shape, dtype, name=name, align_bytes=64, offset=kib * 1024)

        def bank(i, name):
            return psum.tile([P, PASS], F32, name=name, tag="bank%d" % i)

        def load_list(src, name):
            held = lists.tile(list(src.shape), U16, name=name)
            nc.sync.dma_start(held[:], src)
            return held

        def entries(held, first, count):
            return held[:, first // PER_COL : (first + count) // PER_COL]

        def quantise_weight(rows, name, codes):
            raw = tile([P, PACK, PASS], F32, name + "_raw", tag="w_raw", bufs=4)
            nc.sync.dma_start(raw[:], rows.rearrange("(p j) c -> p j c", j=PACK))
            rounded = tile([P, PASS * PACK], BF16, name + "_bf", tag="w_bf", bufs=4)
            nc.scalar.copy(
                rounded[:].rearrange("p (t m j) -> p t m j", t=PACK, j=PACK),
                raw[:].rearrange("p j (m t) -> p t m j", t=PACK),
            )
            scales = tile([P, PASS], U8, name + "_scales")
            nc.vector.quantize_mx(out=codes[:].bitcast(FP8X4), scales=scales[:], in_=rounded[:])
            return codes, scales

        def interleave(dst, src, first, count):
            nc.scalar.copy(
                dst[:, PACK * first : PACK * (first + count)].rearrange("p (c i t) -> p c t i", i=4, t=PACK),
                src[:, :, first : first + count].rearrange("p t (c i) -> p c t i", i=4),
            )

        def load_table(a):
            words = placed([P, T], U32, "tab%d" % a, 16 * a)
            nc.sync.dma_start(words[:].bitcast(I32), tab_words[a].rearrange("p t i -> p (t i)").bitcast(I32))
            return words

        def load_gain(vec, name):
            groups = vec.shape[0] // PASS
            held = tile([P, groups, PACK], F32, name)
            nc.sync.dma_start(held[:], vec.rearrange("(b p t) -> p b t", b=groups, t=PACK))
            return held

        idx = load_list(offs, "idx")
        w2_s_raw = tile([P, H], U8, "w2_s_raw")
        nc.gpsimd.memset(w2_s_raw[:].bitcast(I32), 0)
        tab_s = tile([P, T], U8, "tab_s")
        nc.vector.memset(tab_s[:].bitcast(I32), 0)
        for q in range(4):
            nc.gpsimd.dma_start(
                tab_s[32 * q : 32 * q + 12, :].bitcast(I32), tab_scales[:, 4 * q : 4 * q + 4, :].bitcast(I32)
            )

        def quantise_w1(a):
            name = "w1_%d" % a
            return quantise_weight(w1[a * PASS : (a + 1) * PASS, :], name, tile([P, PASS], U32, name + "_codes"))

        w1_q = [quantise_w1(0), quantise_w1(1)]
        w2_raw = tile([P, 2 * H], U8, "w2_raw")
        nc.sync.dma_start(w2_raw[:].bitcast(I32), w2_words[0].bitcast(I32))
        for q in range(4):
            nc.sync.dma_start(
                w2_s_raw[32 * q : 32 * q + 4, :].bitcast(I32), w2_scales[0, 4 * q : 4 * q + 4, :].bitcast(I32)
            )
        tab = [load_table(0)]
        w1_q.append(quantise_w1(2))
        tab.append(load_table(1))
        tab.append(load_table(2))
        g1_t = load_gain(g1, "g1_t")

        v_s = tile([P, S], U8, "v_s")
        nc.vector.tensor_copy(v_s[:], tab_s[:].indirect(idx[:]))
        v = [tile([P, S], U32, "v0", tag="tab_s")]
        nc.vector.tensor_copy(v[0][:], tab[0][:].indirect(idx[:]))
        v.append(placed([P, S], U32, "v1", 12))
        nc.vector.tensor_copy(v[1][:], tab[1][:].indirect(idx[:]))
        v.append(placed([P, S], U32, "v2", 28))
        for first in (0, HALF):
            nc.vector.tensor_copy(v[2][:, first : first + HALF], tab[2][:].indirect(entries(idx, first, HALF)))

        w2_c = tile([P, 2 * H], U8, "w2_c")
        nc.vector.tensor_copy(
            w2_c[:].rearrange("p (b t m e) -> p b t m e", b=2, t=PACK, e=2),
            w2_raw[:].rearrange("p (b m t e) -> p b t m e", b=2, t=PACK, e=2),
        )
        w2_s = tile([P, H], U8, "w2_s")
        nc.vector.tensor_copy(
            w2_s[:].rearrange("p (b t m) -> p b t m", b=2, t=PACK),
            w2_s_raw[:].rearrange("p (b m t) -> p b t m", b=2, t=PACK),
        )

        def first_product(dst, a, t, first, count, start, stop):
            codes, scales = w1_q[a]
            nc.tensor.matmul_mx(
                out=dst,
                lhsT=codes[:, t * P : (t + 1) * P].bitcast(FP8X4),
                lhsT_scale=scales[:, t * P : (t + 1) * P],
                rhs=v[a][:, first : first + count].bitcast(FP8X4),
                rhs_scale=v_s[4 * a : P, first : first + count],
                start=start,
                stop=stop,
            )

        early = [bank(i, "early%d" % i) for i in range(4)]
        late = [bank(4 + t, "late%d" % t) for t in range(PACK)]
        for a in range(3):
            for i in range(4):
                for t in range(PACK):
                    first_product(
                        early[i][:, t * PIECE : (t + 1) * PIECE], a, t, i * PIECE, PIECE,
                        start=(a == 0 and t == 0), stop=(a == 2 and t == PACK - 1),
                    )
            for t in range(PACK):
                first_product(late[t][:], a, t, HALF, HALF, start=(a == 0), stop=(a == 2))

        idx2 = load_list(offs2, "idx2")
        wgs_t = {}
        pages = {}

        def load_wgs(t, first, count):
            if first == 0:
                wgs_t[t] = tile([P, S], F32, "wgs%d" % t)
            rows = wgs.rearrange("(m t) s -> t m s", t=PACK)[t]
            for q in range(4):
                nc.sync.dma_start(wgs_t[t][32 * q : 32 * q + 32, first : first + count], rows[:, first : first + count])

        def load_page(i):
            b, t = ORDER[i]
            pages[i] = tile([P, T2], F32, "page%d" % i)
            nc.sync.dma_start(pages[i][:], page0.rearrange("(b p t) c -> b t p c", b=2, t=PACK)[b, t])

        load_wgs(0, 0, HALF)
        load_page(0)
        load_page(1)
        load_wgs(1, 0, HALF)
        load_page(2)
        load_wgs(0, HALF, HALF)
        load_wgs(1, HALF, HALF)
        idx3 = load_list(offs3, "idx3")
        idx4 = load_list(offs4, "idx4")
        gs_t, gp_t, gl_t = load_gain(gs, "gs_t"), load_gain(gp, "gp_t"), load_gain(gl, "gl_t")

        f_c = tile([P, S], U32, "f_c")
        f_s = tile([P, S], U8, "f_s")
        f_early = tile([P, HALF * PACK], BF16, "f_early", tag="woven0")
        h = [placed([P, S], F32, "h%d" % i, 4 * i) for i in range(8)]

        def early_piece(i):
            th = tile([P, PIECE, PACK], F32, "th%d" % i, tag="act", bufs=2)
            nc.scalar.activation(th[:], early[i][:].rearrange("p (t n) -> p n t", t=PACK), ACT.Tanh)
            nc.vector.tensor_tensor(
                f_early[:, i * PIECE * PACK : (i + 1) * PIECE * PACK].rearrange("p (n t) -> p n t", t=PACK),
                th[:],
                g1_t[:, 0, :].unsqueeze(1).to_broadcast([P, PIECE, PACK]),
                ALU.mult,
            )

        def quantise_f(src, first, count):
            nc.vector.quantize_mx(
                out=f_c[:, first : first + count].bitcast(FP8X4), scales=f_s[:, first : first + count], in_=src
            )

        def second_product(i, first, count, slot):
            b, t = ORDER[i]
            col = (b * PACK + t) * P
            acc = bank(slot, "h%d_%d" % (i, first))
            nc.tensor.matmul_mx(
                out=acc[:, 0:count],
                lhsT=w2_c[:, 2 * col : 2 * (col + P)].bitcast(FP4X4),
                lhsT_scale=w2_s[:, col : col + P],
                rhs=f_c[:, first : first + count].bitcast(FP8X4),
                rhs_scale=f_s[:, first : first + count],
                start=True,
                stop=True,
            )
            nc.scalar.copy(h[i][:, first : first + count], acc[:, 0:count])

        def put(i, first, count):
            nc.vector.tensor_tensor(
                pages[i][:].indirect(entries(idx2, first, count)),
                h[i][:, first : first + count],
                wgs_t[ORDER[i][1]][:, first : first + count],
                ALU.mult,
            )

        quarter = HALF // 2
        for half in range(2):
            early_piece(2 * half)
            early_piece(2 * half + 1)
            quantise_f(f_early[:, half * quarter * PACK : (half + 1) * quarter * PACK], half * quarter, quarter)
            second_product(0, half * quarter, quarter, half)
        second_product(1, 0, HALF, 2)
        second_product(2, 0, HALF, 3)

        th_late = tile([P, PACK, HALF], F32, "th_late", tag="planes")
        f_planes = tile([P, PACK, HALF], BF16, "f_planes")
        f_late = tile([P, HALF * PACK], BF16, "f_late", tag="woven1")
        for t in range(PACK):
            nc.scalar.activation(th_late[:, t, :], late[t][:], ACT.Tanh)
        for t in range(PACK):
            nc.scalar.activation(f_planes[:, t, :], th_late[:, t, :], ACT.Copy, scale=g1_t[:, 0, t : t + 1])
        for half in range(2):
            interleave(f_late, f_planes, half * quarter, quarter)

        put(0, 0, quarter)
        put(0, quarter, quarter)
        put(1, 0, HALF)
        put(2, 0, HALF)
        quantise_f(f_late[:], HALF, HALF)
        for i in range(3):
            second_product(i, HALF, HALF, 4 + i)
        for i in range(3, 8):
            second_product(i, 0, HALF, (2 * i) % 8)
            second_product(i, HALF, HALF, (2 * i + 1) % 8)

        put(0, HALF, HALF)
        put(1, HALF, HALF)

        x_planes = tile([P, 2, PACK, PICK], BF16, "x_planes", tag="planes")
        x_s = tile([P, 2, PICK], U8, "x_s")
        w3_q = {}
        y = {}

        def pick(i):
            b, t = ORDER[i]
            picked = placed([P, PICK], F32, "picked%d" % i, 4 * (i + 1) if i < 7 else 44)
            nc.vector.tensor_copy(picked[:], pages[i][:].indirect(idx3[:]))
            act = tile([P, PICK], F32, "silu%d" % i, tag="act", bufs=2)
            nc.scalar.activation(act[:], picked[:], ACT.Silu, scale=gs_t[:, b, t : t + 1])
            nc.scalar.activation(x_planes[:, b, t, :], act[:], ACT.Copy, scale=gp_t[:, b, t : t + 1])

        def quantise_w3(b, c, codes):
            rows = w3[b * PASS : (b + 1) * PASS, c * PASS : (c + 1) * PASS]
            w3_q[b, c] = quantise_weight(rows, "w3_%d%d" % (b, c), codes)

        def third_product(b, x_c):
            woven = tile([P, PICK * PACK], BF16, "x_woven%d" % b, tag="woven%d" % b)
            for half in range(2):
                interleave(woven, x_planes[:, b, :, :], half * quarter, quarter)
            nc.vector.quantize_mx(out=x_c[:].bitcast(FP8X4), scales=x_s[:, b, :], in_=woven[:])
            for i, (c, t) in enumerate(ORDER):
                if b == 0:
                    y[i] = bank(i, "y%d" % i)
                codes, scales = w3_q[b, c]
                nc.tensor.matmul_mx(
                    out=y[i][:],
                    lhsT=codes[:, t * P : (t + 1) * P].bitcast(FP8X4),
                    lhsT_scale=scales[:, t * P : (t + 1) * P],
                    rhs=x_c[:].bitcast(FP8X4),
                    rhs_scale=x_s[:, b, :],
                    start=(b == 0),
                    stop=(b == 1),
                )

        pick(0)
        put(2, HALF, HALF)
        pick(1)
        quantise_w3(0, 0, placed([P, PASS], U32, "w3_00_codes", 4 * 3 + 2))
        quantise_w3(0, 1, placed([P, PASS], U32, "w3_01_codes", 4 * 4 + 2))
        quantise_w3(1, 0, placed([P, PASS], U32, "w3_10_codes", 4 * 5 + 2))
        quantise_w3(1, 1, placed([P, PASS], U32, "w3_11_codes", 4 * 6 + 2))
        load_wgs(2, 0, S)
        load_page(3)
        load_wgs(3, 0, S)
        for i in range(4, 8):
            load_page(i)
        for i in range(3, 8):
            put(i, 0, S)
            pick(i - 1)
        third_product(0, tile([P, PICK], U32, "x_c0", tag="wgs2"))
        pick(7)
        third_product(1, tile([P, PICK], U32, "x_c1"))

        settled_a = placed([P, 6, PICK], F32, "settled_a", 30)
        settled_b = tile([P, 2, PICK], F32, "settled_b", tag="woven1")
        result = placed([P, 8, PICK], F32, "result", 0)

        def settled(i):
            return settled_a[:, i, :] if i < 6 else settled_b[:, i - 6, :]

        for i in range(8):
            nc.vector.tensor_copy(settled(i), pages[i][:].indirect(idx4[:]))
        for i, (c, t) in enumerate(ORDER):
            nc.vector.scalar_tensor_tensor(
                result[:, i, :], settled(i), gl_t[:, c, t : t + 1], y[i][:], ALU.mult, ALU.min
            )
            nc.sync.dma_start(out.rearrange("(c p t) j -> c t p j", c=2, t=PACK)[c, t], result[:, i, :])
